import numpy as np
import ml_dtypes


def mxq(x, axis, fmt="e4m3"):
    dtype, down = {"e4m3": (ml_dtypes.float8_e4m3fn, 7), "e5m2": (ml_dtypes.float8_e5m2, 14)}[fmt]
    v = np.moveaxis(np.asarray(x, np.float32).astype(ml_dtypes.bfloat16).astype(np.float64), axis, -1)
    blocks = v.reshape(v.shape[:-1] + (-1, 32))
    amax = np.abs(blocks).max(-1, keepdims=True)
    byte = np.maximum(np.where(amax > 0, np.frexp(amax)[1] - 1 + 127, 0) - down, 1)
    scale = np.exp2(byte - 127.0)
    codes = (blocks / scale).astype(np.float32).astype(dtype).astype(np.float64)
    return np.moveaxis((codes * scale).reshape(v.shape), -1, axis)


WIDE = False


def mx_kscale(k):
    if not WIDE:
        return np.ones(k)
    levels = np.array([10, -10, 5, -5, 0])
    if k % 512:
        return np.exp2(np.random.permutation(np.resize(levels, k // 32))).repeat(32)
    a = np.empty((k // 512, 16))
    for p in range(k // 512):
        a[p, :8] = np.random.permutation(np.resize(levels, 8))
        for g in range(8):
            far = levels[np.abs(levels - a[p, g]) >= 10]
            a[p, g + 8] = far[np.random.randint(len(far))]
    return np.exp2(a.ravel()).repeat(32)


def f64(x):
    return np.asarray(x).astype(np.float64)


def striped(idx):
    return np.tile(idx.reshape(-1, 16).T, (8, 1)).astype(np.uint16)


def unstriped(offs):
    return offs[:16].T.reshape(-1).astype(np.int64)


E2M1 = np.array([0.0, 0.5, 1.0, 1.5, 2.0, 3.0, 4.0, 6.0, -0.0, -0.5, -1.0, -1.5, -2.0, -3.0, -4.0, -6.0])


def pack_weight(w, fmt):
    k, n = w.shape
    w = f64(np.asarray(w, np.float32).astype(ml_dtypes.bfloat16)).reshape(k // 32, 32, n)
    amax = np.abs(w).max(1)
    if fmt == "e4m3":
        byte = np.frexp(amax)[1] - 1 + 127 - 7
    else:
        mant, ex = np.frexp(amax / 6.0)
        byte = np.where(mant > 0.5, ex, ex - 1) + 127
    byte = np.clip(np.where(amax > 0, byte, 1), 1, 254)
    scaled = (w * np.exp2(127.0 - byte)[:, None, :]).reshape(k, n).astype(np.float32)
    by_word = np.ascontiguousarray(scaled.reshape(k // 512, 128, 4, n).transpose(0, 1, 3, 2))
    if fmt == "e4m3":
        words = by_word.astype(ml_dtypes.float8_e4m3fn).view(np.uint8)
    else:
        c = by_word.astype(ml_dtypes.float4_e2m1fn).view(np.uint8) & 0xF
        words = (c[..., 0::2] | (c[..., 1::2] << 4)).reshape(k // 512, 128, 2 * n)
    return np.ascontiguousarray(words), np.ascontiguousarray(byte.astype(np.uint8).reshape(k // 512, 16, n))


def unpack_weight(words, scales, fmt):
    g, _, n = scales.shape
    words = np.ascontiguousarray(words).reshape(g, 128, n, -1)
    if fmt == "e4m3":
        vals = words.view(ml_dtypes.float8_e4m3fn).astype(np.float64)
    else:
        nib = np.empty((g, 128, n, 4), np.uint8)
        nib[..., 0::2] = words & 0xF
        nib[..., 1::2] = words >> 4
        vals = E2M1[nib]
    vals = vals * np.repeat(np.exp2(scales.astype(np.float64) - 127.0), 8, axis=1)[..., None]
    return vals.transpose(0, 1, 3, 2).reshape(g * 512, n)


def gelu(v):
    return 0.5 * v * (1.0 + np.tanh(np.sqrt(2.0 / np.pi) * (v + 0.044715 * v**3)))


def often(T, S):
    return np.random.permutation(T)[(T * np.random.uniform(0, 1, S) ** 4).astype(np.int64)]


def bf(x):
    return np.asarray(x, np.float32).astype(ml_dtypes.bfloat16)


def planes(Y):
    n, m = Y.shape
    b = f64(bf(Y)).reshape(n // 32, 32, m)
    amax = np.abs(b).max(1)
    byte = np.clip(np.where(amax > 0, np.frexp(amax)[1] - 1 + 127 - 7, 1), 1, 254)
    codes = (b * np.exp2(127.0 - byte)[:, None, :]).reshape(n, m).astype(np.float32).astype(ml_dtypes.float8_e4m3fn).view(np.uint8)
    words = codes.reshape(n // 512, 128, 4, m).transpose(0, 1, 3, 2)
    return np.ascontiguousarray(words), np.ascontiguousarray(byte.astype(np.uint8).reshape(n // 512, 16, m))


K, K2, H, N, T, S, P = 1024, 512, 1024, 512, 4096, 1024, 512


def setup_inputs():
    n = np.random.standard_normal
    s, s2, u = mx_kscale(K)[:, None], mx_kscale(K2)[:, None], mx_kscale(H)[:, None]
    d = {}
    d["tab_words"], d["tab_scales"] = pack_weight(n((K, T)) * s, "e4m3")
    d["tab2_words"], d["tab2_scales"] = pack_weight(n((K2, T)) * s2, "e4m3")
    d["tab3_words"], d["tab3_scales"] = pack_weight(n((K2, T)) * s2, "e4m3")
    d["offs"] = striped(np.random.permutation(T)[:S])
    d["offs2"] = striped(np.random.permutation(T)[:S])
    d["offs3"] = striped(np.random.permutation(T)[:S])
    d["pos1"] = striped(np.random.permutation(S)[:P])
    d["pos2"] = striped(often(S, P))
    d["pos3"] = striped(often(S, P))
    d["wk_words"], d["wk_scales"] = pack_weight(5.0 * n((K, H)) / K**0.5 / s, "e2m1")
    d["wl"] = (n((K2, H)) / K2**0.5 / s2 * u.T).astype(np.float32)
    d["we"] = (n((K2, H)) / K2**0.5 / s2 * u.T).astype(np.float32)
    d["wy"] = (0.5 * n((H, N)) / H**0.5 / u * np.exp(0.8 * n(N))).astype(np.float32)
    d["wt_words"], d["wt_scales"] = pack_weight(0.6 * n((H, N)) / H**0.5 / u, "e2m1")
    return d


def reference(tab_words, tab_scales, tab2_words, tab2_scales, tab3_words, tab3_scales,
              offs, offs2, offs3, pos1, pos2, pos3, wk_words, wk_scales, wl, we, wy, wt_words, wt_scales):
    v = unpack_weight(tab_words, tab_scales, "e4m3")[:, unstriped(offs)]
    v2 = unpack_weight(tab2_words, tab2_scales, "e4m3")[:, unstriped(offs2)]
    v3 = unpack_weight(tab3_words, tab3_scales, "e4m3")[:, unstriped(offs3)]
    a = unpack_weight(wk_words, wk_scales, "e2m1").T @ v
    b = mxq(f64(wl), 0, "e4m3").T @ v2
    d = mxq(f64(we), 0, "e4m3").T @ v3
    z = np.sqrt(1.0 + np.abs(a[:, unstriped(pos1)])) * b[:, unstriped(pos2)] - d[:, unstriped(pos3)]
    zq = mxq(z, 0, "e4m3")
    lin = mxq(f64(wy), 0, "e4m3").T @ zq
    bent = unpack_weight(wt_words, wt_scales, "e2m1").T @ zq
    y = lin + np.tanh(bent)
    words, scales = planes(y)
    return y, words, scales

@@ -1,0 +1,367 @@
+from contextlib import ExitStack
+
+import concourse.mybir as mybir
+
+F32 = mybir.dt.float32
+BF16 = mybir.dt.bfloat16
+I32 = mybir.dt.int32
+U32 = mybir.dt.uint32
+U16 = mybir.dt.uint16
+U8 = mybir.dt.uint8
+FP8X4 = mybir.dt.float8_e4m3fn_x4
+FP4X4 = mybir.dt.float4_e2m1fn_x4
+ACT = mybir.ActivationFunctionType
+ALU = mybir.AluOpType
+
+FLOPS = 5368709120
+P = 128
+T = 4096
+S = 1024
+NJ = 512
+PARTS = [256,128,128]
+MULT_ENG = "v"
+SUB_ENG = "v"
+W_ENG = ["v","s","s","s","v","s"]
+W_ORDER = "q j t"
+GA_BUFS = 4
+RES_BUFS = 9
+
+
+def tile_list_peanut_ejector_join_kernel(
+    tc, tab_words, tab_scales, tab2_words, tab2_scales, tab3_words, tab3_scales,
+    offs, offs2, offs3, pos1, pos2, pos3, wk_words, wk_scales, wl, we, wy, wt_words, wt_scales,
+    out_0, out_1, out_2,
+):
+    nc = tc.nc
+    with ExitStack() as ctx:
+        keep = ctx.enter_context(tc.tile_pool(name="keep", bufs=1))
+        ring = ctx.enter_context(tc.tile_pool(name="ring", bufs=2))
+        placed = ctx.enter_context(tc.tile_pool(name="placed", bufs=1))
+        psum = ctx.enter_context(tc.psum_pool(name="psum", bufs=8))
+
+        def load_list(src, name):
+            t = keep.tile([P, src.shape[1]], U16, name=name)
+            nc.sync.dma_start(t[:], src)
+            return t
+
+        def zeroed(width, name):
+            t = keep.tile([P, width], U8, name=name, align_bytes=64)
+            nc.vector.memset(t[:].bitcast(I32), 0)
+            return t
+
+        def load_words(src, name, slot):
+            t = placed.tile([P, T], I32, name=name, align_bytes=64, offset=16384 * slot)
+            nc.sync.dma_start(t[:], src.rearrange("p n t -> p (n t)").bitcast(I32))
+            return t
+
+        def load_raw(src, name):
+            t = ring.tile([P, 4, 512], F32, name=name, tag="raw", bufs=3, align_bytes=64)
+            nc.sync.dma_start(t[:], src.rearrange("(p j) c -> p j c", j=4))
+            return t
+
+        def load_scale_rows(queue, dst, first, src):
+            rows = 4 * src.shape[0]
+            for q in range(4):
+                queue.dma_start(dst[32 * q + first : 32 * q + first + rows, :].bitcast(I32),
+                                src[:, 4 * q : 4 * q + 4, :].bitcast(I32))
+
+        def shifted(dst, src, k):
+            nc.sync.dma_start(dst[0:112, :].bitcast(I32), src[k : k + 112, :].bitcast(I32))
+
+        def deal(dst, src, groups):
+            nc.vector.tensor_copy(dst.bitcast(U16).rearrange("p (g t q) -> p g t q", g=groups, t=4),
+                                  src.bitcast(U16).rearrange("p (g q t) -> p g t q", g=groups, t=4))
+
+        def gather_words(win, lst, name):
+            g = keep.tile([P, S], U32, name=name, align_bytes=64)
+            nc.vector.tensor_copy(g[:], win[:].bitcast(U32).indirect(lst[:]))
+            return g
+
+        def gather_bytes(win, lst, name):
+            g = keep.tile([P, S], U8, name=name, align_bytes=64)
+            nc.vector.tensor_copy(g[:], win[:].indirect(lst[:]))
+            return g
+
+        def round_weight(raw, name, eng):
+            bf = ring.tile([P, 2048], BF16, name=name + "_bf", tag="wbf", bufs=2, align_bytes=64)
+            dst = bf[:].rearrange("p (t q j) -> p " + W_ORDER, t=4, j=4)
+            src = raw[:].rearrange("p j (q t) -> p " + W_ORDER, t=4)
+            if eng == "s":
+                nc.scalar.copy(dst, src)
+            elif eng == "v":
+                nc.vector.tensor_copy(dst, src)
+            else:
+                nc.gpsimd.tensor_scalar(dst, src, 1.0, 0.0, ALU.mult, ALU.add)
+            return bf
+
+        def quantize(bf, name, width):
+            codes = keep.tile([P, width], U32, name=name + "_codes", align_bytes=64)
+            scales = keep.tile([P, width], U8, name=name + "_scales", align_bytes=64)
+            nc.vector.quantize_mx(out=codes[:].bitcast(FP8X4), scales=scales[:], in_=bf)
+            return codes, scales
+
+        def first_stage(name, passes):
+            res = ring.tile([P, S], F32, name=name, tag="res", bufs=RES_BUFS, align_bytes=64)
+            for h in range(2):
+                cols = slice(512 * h, 512 * (h + 1))
+                bank = psum.tile([P, 512], F32, name=name + "_bank", tag="bank")
+                for i, (w, ws, v, vs) in enumerate(passes):
+                    nc.tensor.matmul_mx(out=bank[:], lhsT=w, lhsT_scale=ws, rhs=v[:, cols].bitcast(FP8X4),
+                                        rhs_scale=vs[:, cols], start=(i == 0), stop=(i == len(passes) - 1))
+                nc.scalar.copy(res[:, cols], bank[:])
+            return res
+
+        def load_planes(queue, dst, src):
+            for q in range(4):
+                queue.dma_start(dst[32 * q : 32 * q + 4, :].bitcast(I32).rearrange("r (a c) -> r a c", a=2),
+                                src[:, 4 * q : 4 * q + 4, :].bitcast(I32).rearrange("a r c -> r a c"))
+
+        warm = keep.tile([P, 1], F32, name="warm")
+        nc.vector.memset(warm[:], 1.0)
+        nc.scalar.activation(warm[:], warm[:], ACT.Sqrt)
+        s2_win = zeroed(T, "s2_win")
+        s1_win = zeroed(T, "s1_win")
+        s3_win = zeroed(T, "s3_win")
+        ws_raw = zeroed(3072, "ws_raw")
+        v_sc1 = zeroed(S, "v_sc1")
+        l_offs2 = load_list(offs2, "l_offs2")
+        wl_raw0 = load_raw(wl[:, 0:512], "wl_raw0")
+        load_scale_rows(nc.sync, s2_win, 0, tab2_scales)
+        w2_win = load_words(tab2_words[0], "w2_win", 0)
+        l_offs = load_list(offs, "l_offs")
+        load_scale_rows(nc.sync, s1_win, 0, tab_scales)
+        wl_raw1 = load_raw(wl[:, 512:1024], "wl_raw1")
+        l_pos2 = load_list(pos2, "l_pos2")
+        l_offs3 = load_list(offs3, "l_offs3")
+        wk_raw = ring.tile([P, 2, 2048], U8, name="wk_raw", tag="y", bufs=2, align_bytes=64)
+        nc.sync.dma_start(wk_raw[:].bitcast(I32), wk_words.rearrange("a p c -> p a c").bitcast(I32))
+        load_planes(nc.sync, ws_raw[:, 0:2048], wk_scales)
+        w1_win0 = load_words(tab_words[0], "w1_win0", 1)
+        wl_bf0 = round_weight(wl_raw0, "wl0", W_ENG[0])
+        wl_q = [quantize(wl_bf0[:], "wl0", 512)]
+        v2_sc = gather_bytes(s2_win, l_offs2, "v2_sc")
+        v2 = gather_words(w2_win, l_offs2, "v2")
+        v_sc0 = gather_bytes(s1_win, l_offs, "v_sc0")
+        shifted(v_sc1, v_sc0, 4)
+        load_planes(nc.sync, ws_raw[:, 2048:3072], wt_scales)
+        w1_win1 = load_words(tab_words[1], "w1_win1", 2)
+        l_pos1 = load_list(pos1, "l_pos1")
+        load_scale_rows(nc.sync, s3_win, 0, tab3_scales)
+        we_raw = [load_raw(we[:, 0:512], "we_raw0")]
+        wl_bf1 = round_weight(wl_raw1, "wl1", W_ENG[1])
+        wl_q.append(quantize(wl_bf1[:], "wl1", 512))
+        wk_dealt = keep.tile([P, 4096], U8, name="wk_dealt", align_bytes=64)
+        deal(wk_dealt[:], wk_raw[:].rearrange("p a c -> p (a c)"), 4)
+        ws_dealt = keep.tile([P, 3072], U8, name="ws_dealt", align_bytes=64)
+        nc.vector.tensor_copy(ws_dealt[:].rearrange("p (b t q) -> p b t q", b=6, t=4),
+                              ws_raw[:].rearrange("p (b q t) -> p b t q", b=6, t=4))
+        w3_win = load_words(tab3_words[0], "w3_win", 0)
+        we_raw.append(load_raw(we[:, 512:1024], "we_raw1"))
+        l_pos3 = load_list(pos3, "l_pos3")
+        wt_raw = ring.tile([P, 2, 1024], U8, name="wt_raw", tag="y", bufs=2, align_bytes=64)
+        nc.sync.dma_start(wt_raw[:].bitcast(I32), wt_words.rearrange("a p c -> p a c").bitcast(I32))
+
+        def plain_pass(wq, s, v, vs):
+            codes, scales = wq[s // 4]
+            cols = slice(128 * (s % 4), 128 * (s % 4 + 1))
+            return [(codes[:, cols].bitcast(FP8X4), scales[:, cols], v, vs)]
+
+        prod = [keep.tile([P, 4, NJ], F32, name="prod0", align_bytes=64)]
+        v1 = []
+        def pick_b(s):
+            res = first_stage("b%d" % s, plain_pass(wl_q, s, v2, v2_sc))
+            nc.vector.tensor_copy(prod[s // 4][:, s % 4, :], res[:].indirect(l_pos2[:]))
+
+        for s in range(4):
+            pick_b(s)
+        v1.append(gather_words(w1_win0, l_offs, "v1_0"))
+        v1.append(gather_words(w1_win1, l_offs, "v1_1"))
+        prod.append(placed.tile([P, 4, NJ], F32, name="prod1", align_bytes=64, offset=28672))
+        for s in range(4, 8):
+            pick_b(s)
+        we_q = [quantize(round_weight(we_raw[0], "we0", W_ENG[2])[:], "we0", 512)]
+        wy_raw = [load_raw(wy[512 * a : 512 * (a + 1), :], "wy_raw%d" % a) for a in range(2)]
+
+        def a_passes(s):
+            out = []
+            for a in range(2):
+                first = 2048 * a + 256 * s
+                plane = ws_dealt[:, 1024 * a : 1024 * (a + 1)]
+                out.append((wk_dealt[:, first : first + 256].bitcast(FP4X4), plane[:, 128 * s : 128 * (s + 1)],
+                            v1[a], (v_sc0, v_sc1)[a]))
+            return out
+
+        picked = {}
+        d_res = {}
+        wy_q = []
+
+        def pick_a(s):
+            res = first_stage("a%d" % s, a_passes(s))
+            picked[s] = ring.tile([P, NJ], F32, name="ga%d" % s, tag="ga", bufs=GA_BUFS, align_bytes=64)
+            nc.vector.tensor_copy(picked[s][:], res[:].indirect(l_pos1[:]))
+
+        def root(s):
+            nc.scalar.activation(picked[s][:], picked[s][:], ACT.Abs)
+            nc.scalar.activation(picked[s][:], picked[s][:], ACT.Sqrt, bias=1.0)
+
+        def mult(s):
+            dst = prod[s // 4][:, s % 4, :]
+            eng = nc.vector if MULT_ENG == "v" else nc.gpsimd
+            eng.tensor_tensor(dst, dst, picked[s][:], ALU.mult)
+
+        def make_d(s):
+            d_res[s] = first_stage("d%d" % s, plain_pass(we_q, s, v3, v3_sc))
+
+        def make_wy(a):
+            wy_q.append(quantize(round_weight(wy_raw[a], "wy%d" % a, W_ENG[4 + a])[:], "wy%d" % a, 512))
+
+        gd_tiles = {}
+
+        def pick_d(s, first, w):
+            key = (s // 4, first)
+            if key not in gd_tiles:
+                gd_tiles[key] = ring.tile([P, 4, w], F32, name="gd%d_%d" % key, tag="gd0" if w == 512 else "gdp",
+                                          bufs=1 if w == 512 else 1, align_bytes=64)
+            nc.vector.tensor_copy(gd_tiles[key][:, s % 4, :],
+                                  d_res[s][:].indirect(l_pos3[:, first // 16 : (first + w) // 16]))
+
+        def join(g, first, w):
+            gd = gd_tiles[(g, first)]
+            zbf = ring.tile([P, w, 4], BF16, name="zbf%d_%d" % (g, first), tag="wbf", bufs=2, align_bytes=64)
+            if SUB_ENG == "v":
+                nc.vector.tensor_tensor(
+                    zbf[:].rearrange("p (c i) t -> p c t i", i=2),
+                    prod[g][:, :, first : first + w].rearrange("p t (c i) -> p c t i", i=2),
+                    gd[:].rearrange("p t (c i) -> p c t i", i=2), ALU.subtract)
+            else:
+                nc.gpsimd.tensor_tensor(gd[:], prod[g][:, :, first : first + w], gd[:], ALU.subtract)
+                nc.scalar.copy(zbf[:].rearrange("p (c i) t -> p c t i", i=4),
+                               gd[:].rearrange("p t (c i) -> p c t i", i=4))
+            return zbf
+
+        def quantize_z(zbf, g, first, w):
+            return quantize(zbf[:].rearrange("p j t -> p (j t)"), "z%d_%d" % (g, first), w)
+
+        wt_dealt = keep.tile([P, 2048], U8, name="wt_dealt", align_bytes=64)
+        y_codes = keep.tile([P, NJ], U32, name="y_codes", align_bytes=64)
+        y_scales = keep.tile([P, NJ], U8, name="y_scales", align_bytes=64)
+        y_rows = out_0.rearrange("(p t) j -> p t j", t=4)
+        words_out = out_1[0].rearrange("p j t -> p (j t)").bitcast(I32)
+
+        banks = {}
+
+        def second_passes(part, w, g, codes, scales, col):
+            per_bank = 512 // w
+            for t0 in range(0, 4, per_bank):
+                if g == 0:
+                    banks[(part, t0)] = (psum.tile([P, 512], F32, name="bent", tag="bank"),
+                                         psum.tile([P, 512], F32, name="lin", tag="bank"))
+                bent = banks[(part, t0)][0]
+                for t in range(t0, t0 + per_bank):
+                    for c0 in range(0, w, 128):
+                        o = (t - t0) * w + c0
+                        byte = 1024 * g + 256 * t
+                        nc.tensor.matmul_mx(
+                            out=bent[:, o : o + 128], lhsT=wt_dealt[:, byte : byte + 256].bitcast(FP4X4),
+                            lhsT_scale=ws_dealt[:, 2048 + 512 * g + 128 * t : 2048 + 512 * g + 128 * (t + 1)],
+                            rhs=codes[:, col + c0 : col + c0 + 128].bitcast(FP8X4),
+                            rhs_scale=scales[:, col + c0 : col + c0 + 128],
+                            start=(g == 0 and o == 0), stop=(g == 1 and o == 384))
+            for t0 in range(0, 4, per_bank):
+                lin = banks[(part, t0)][1]
+                for t in range(t0, t0 + per_bank):
+                    o = (t - t0) * w
+                    nc.tensor.matmul_mx(
+                        out=lin[:, o : o + w], lhsT=wy_q[g][0][:, 128 * t : 128 * (t + 1)].bitcast(FP8X4),
+                        lhsT_scale=wy_q[g][1][:, 128 * t : 128 * (t + 1)],
+                        rhs=codes[:, col : col + w].bitcast(FP8X4), rhs_scale=scales[:, col : col + w],
+                        start=(g == 0 and o == 0), stop=(g == 1 and o + w == 512))
+
+        def second_stage(part, first, w, last):
+            y = ring.tile([P, 4, w], F32, name="y%d" % part, tag="y", bufs=2, align_bytes=64)
+            per_bank = 512 // w
+            flat = y[:].rearrange("p t j -> p (t j)")
+            for t0 in range(0, 4, per_bank):
+                bent, lin = banks[(part, t0)]
+                cols = slice(t0 * w, t0 * w + 512)
+                nc.scalar.activation(flat[:, cols], bent[:], ACT.Tanh)
+                nc.vector.tensor_tensor(flat[:, cols], lin[:], flat[:, cols], ALU.add)
+            nc.sync.dma_start(y_rows[:, :, first : first + w], y[:])
+            ybf = ring.tile([P, w, 4], BF16, name="ybf%d" % part, tag="ybf", bufs=2, align_bytes=64)
+            dst = ybf[:].rearrange("p (c i) t -> p c t i", i=4)
+            src = y[:].rearrange("p t (c i) -> p c t i", i=4)
+            if last:
+                nc.vector.tensor_copy(dst, src)
+            else:
+                nc.scalar.copy(dst, src)
+            nc.vector.quantize_mx(out=y_codes[:, first : first + w].bitcast(FP8X4),
+                                  scales=y_scales[:, first : first + w],
+                                  in_=ybf[:].rearrange("p j t -> p (j t)"))
+            nc.sync.dma_start(words_out[:, first : first + w], y_codes[:, first : first + w].bitcast(I32))
+
+
+        pick_a(0)
+        pick_a(1)
+        v3_sc = gather_bytes(s3_win, l_offs3, "v3_sc")
+        pick_a(2)
+        pick_a(3)
+        root(0)
+        v3 = gather_words(w3_win, l_offs3, "v3")
+        pick_a(4)
+        root(1)
+        mult(0)
+        pick_a(5)
+        root(2)
+        mult(1)
+        we_q.append(quantize(round_weight(we_raw[1], "we1", W_ENG[3])[:], "we1", 512))
+        root(3)
+        mult(2)
+        make_d(0)
+        pick_d(0, 0, 512)
+        make_d(1)
+        pick_d(1, 0, 512)
+        mult(3)
+        pick_a(6)
+        root(4)
+        make_d(2)
+        pick_d(2, 0, 512)
+        make_d(3)
+        pick_d(3, 0, 512)
+        deal(wt_dealt[:], wt_raw[:].rearrange("p a c -> p (a c)"), 2)
+        pick_a(7)
+        root(5)
+        z0 = quantize_z(join(0, 0, 512), 0, 0, 512)
+        mult(4)
+        make_wy(0)
+        make_d(4)
+        root(6)
+        mult(5)
+        make_d(5)
+        root(7)
+        mult(6)
+        make_d(6)
+        mult(7)
+        make_d(7)
+        make_wy(1)
+
+        starts = [sum(PARTS[:i]) for i in range(len(PARTS))]
+        for part, w in enumerate(PARTS):
+            second_passes(part, w, 0, z0[0], z0[1], starts[part])
+        for s in range(4, 8):
+            pick_d(s, 0, PARTS[0])
+        for part, w in enumerate(PARTS):
+            more = part + 1 < len(PARTS)
+            zbf = join(1, starts[part], w)
+            if more:
+                pick_d(4, starts[part + 1], PARTS[part + 1])
+            z1 = quantize_z(zbf, 1, starts[part], w)
+            second_passes(part, w, 1, z1[0], z1[1], 0)
+            if more:
+                for s in range(5, 8):
+                    pick_d(s, starts[part + 1], PARTS[part + 1])
+            if part >= 1:
+                second_stage(part - 1, starts[part - 1], PARTS[part - 1], False)
+        second_stage(len(PARTS) - 1, starts[-1], PARTS[-1], True)
+        for q in range(4):
+            queue = nc.sync if q % 2 == 0 else nc.scalar
+            queue.dma_start(out_2[0, 4 * q : 4 * q + 4, :].bitcast(I32), y_scales[32 * q : 32 * q + 4, :].bitcast(I32))

@@ -14,17 +14,24 @@ ACT = mybir.ActivationFunctionType
 ALU = mybir.AluOpType
 
 FLOPS = 5368709120
+
 P = 128
-T = 4096
-S = 1024
-NJ = 512
-PARTS = [256,128,128]
-MULT_ENG = "v"
-SUB_ENG = "v"
-W_ENG = ["v","s","s","s","v","s"]
-W_ORDER = "q j t"
-GA_BUFS = 4
-RES_BUFS = 9
+PACK = 4
+PASS = P * PACK
+BANK = 512
+TABLE = 4096
+PICKS = 1024
+JOINED = 512
+SLICES = 8
+FP4_N = 128
+PARTS = (256, 128, 128)
+PASS1_ROWS = 16
+
+WINDOW_BYTES = TABLE * 4
+PICKED_BYTES = JOINED * 4
+RESULT_BUFS = 9
+RAW_BUFS = 3
+ALIGN = 64
 
 
 def tile_list_peanut_ejector_join_kernel(
@@ -40,328 +47,284 @@ def tile_list_peanut_ejector_join_kernel(
         psum = ctx.enter_context(tc.psum_pool(name="psum", bufs=8))
 
         def load_list(src, name):
-            t = keep.tile([P, src.shape[1]], U16, name=name)
-            nc.sync.dma_start(t[:], src)
-            return t
+            tile = keep.tile([P, src.shape[1]], U16, name=name)
+            nc.sync.dma_start(tile[:], src)
+            return tile
 
         def zeroed(width, name):
-            t = keep.tile([P, width], U8, name=name, align_bytes=64)
-            nc.vector.memset(t[:].bitcast(I32), 0)
-            return t
+            tile = keep.tile([P, width], U8, name=name, align_bytes=ALIGN)
+            nc.vector.memset(tile[:].bitcast(I32), 0)
+            return tile
 
-        def load_words(src, name, slot):
-            t = placed.tile([P, T], I32, name=name, align_bytes=64, offset=16384 * slot)
-            nc.sync.dma_start(t[:], src.rearrange("p n t -> p (n t)").bitcast(I32))
-            return t
+        def load_window(words, name, place):
+            tile = placed.tile([P, TABLE], I32, name=name, align_bytes=ALIGN, offset=WINDOW_BYTES * place)
+            nc.sync.dma_start(tile[:], words.rearrange("p n t -> p (n t)").bitcast(I32))
+            return tile
 
-        def load_raw(src, name):
-            t = ring.tile([P, 4, 512], F32, name=name, tag="raw", bufs=3, align_bytes=64)
-            nc.sync.dma_start(t[:], src.rearrange("(p j) c -> p j c", j=4))
-            return t
+        def load_weight(rows, name):
+            tile = ring.tile([P, PACK, PASS], F32, name=name, tag="raw", bufs=RAW_BUFS, align_bytes=ALIGN)
+            nc.sync.dma_start(tile[:], rows.rearrange("(p j) c -> p j c", j=PACK))
+            return tile
 
-        def load_scale_rows(queue, dst, first, src):
-            rows = 4 * src.shape[0]
-            for q in range(4):
-                queue.dma_start(dst[32 * q + first : 32 * q + first + rows, :].bitcast(I32),
-                                src[:, 4 * q : 4 * q + 4, :].bitcast(I32))
+        def load_fp4(words, name):
+            tile = ring.tile([P, 2, words.shape[2]], U8, name=name, tag="y", bufs=len(PARTS), align_bytes=ALIGN)
+            nc.sync.dma_start(tile[:].bitcast(I32), words.rearrange("a p c -> p a c").bitcast(I32))
+            return tile
 
-        def shifted(dst, src, k):
-            nc.sync.dma_start(dst[0:112, :].bitcast(I32), src[k : k + 112, :].bitcast(I32))
+        def load_plane(tile, scales):
+            for r in range(4):
+                nc.sync.dma_start(tile[r:P:32, :].bitcast(I32), scales[0, r:16:4, :].bitcast(I32))
 
-        def deal(dst, src, groups):
-            nc.vector.tensor_copy(dst.bitcast(U16).rearrange("p (g t q) -> p g t q", g=groups, t=4),
-                                  src.bitcast(U16).rearrange("p (g q t) -> p g t q", g=groups, t=4))
+        def load_planes_stacked(tile, scales):
+            for r in range(4):
+                nc.sync.dma_start(tile[r:P:PASS1_ROWS, :].bitcast(I32),
+                                  scales[:, r:16:4, :].bitcast(I32).rearrange("a q c -> q a c"))
 
-        def gather_words(win, lst, name):
-            g = keep.tile([P, S], U32, name=name, align_bytes=64)
-            nc.vector.tensor_copy(g[:], win[:].bitcast(U32).indirect(lst[:]))
-            return g
+        def load_planes_beside(tile, scales):
+            for r in range(4):
+                nc.sync.dma_start(tile[r:P:32, :].bitcast(I32).rearrange("q (a c) -> q a c", a=2),
+                                  scales[:, r:16:4, :].bitcast(I32).rearrange("a q c -> q a c"))
 
-        def gather_bytes(win, lst, name):
-            g = keep.tile([P, S], U8, name=name, align_bytes=64)
-            nc.vector.tensor_copy(g[:], win[:].indirect(lst[:]))
-            return g
+        def gather_words(window, entries, name):
+            tile = keep.tile([P, PICKS], U32, name=name, align_bytes=ALIGN)
+            nc.vector.tensor_copy(tile[:], window[:].bitcast(U32).indirect(entries[:]))
+            return tile
 
-        def round_weight(raw, name, eng):
-            bf = ring.tile([P, 2048], BF16, name=name + "_bf", tag="wbf", bufs=2, align_bytes=64)
-            dst = bf[:].rearrange("p (t q j) -> p " + W_ORDER, t=4, j=4)
-            src = raw[:].rearrange("p j (q t) -> p " + W_ORDER, t=4)
-            if eng == "s":
-                nc.scalar.copy(dst, src)
-            elif eng == "v":
-                nc.vector.tensor_copy(dst, src)
-            else:
-                nc.gpsimd.tensor_scalar(dst, src, 1.0, 0.0, ALU.mult, ALU.add)
-            return bf
+        def gather_bytes(window, entries, name):
+            tile = keep.tile([P, PICKS], U8, name=name, align_bytes=ALIGN)
+            nc.vector.tensor_copy(tile[:], window[:].indirect(entries[:]))
+            return tile
 
-        def quantize(bf, name, width):
-            codes = keep.tile([P, width], U32, name=name + "_codes", align_bytes=64)
-            scales = keep.tile([P, width], U8, name=name + "_scales", align_bytes=64)
-            nc.vector.quantize_mx(out=codes[:].bitcast(FP8X4), scales=scales[:], in_=bf)
+        def deal(src, dtype, name):
+            tile = keep.tile([P, src.shape[1]], U8, name=name, align_bytes=ALIGN)
+            nc.vector.tensor_copy(tile[:].bitcast(dtype).rearrange("p (g t q) -> p g t q", t=PACK, q=P),
+                                  src.bitcast(dtype).rearrange("p (g q t) -> p g t q", t=PACK, q=P))
+            return tile
+
+        def quantize(rounded, width, name):
+            codes = keep.tile([P, width], U32, name=name + "_codes", align_bytes=ALIGN)
+            scales = keep.tile([P, width], U8, name=name + "_scales", align_bytes=ALIGN)
+            nc.vector.quantize_mx(out=codes[:].bitcast(FP8X4), scales=scales[:], in_=rounded)
             return codes, scales
 
+        def round_weight(raw, name, on_gpsimd):
+            tile = ring.tile([P, PACK * PASS], BF16, name=name, tag="rounded", align_bytes=ALIGN)
+            if on_gpsimd:
+                nc.gpsimd.tensor_scalar(tile[:].rearrange("p (t q j) -> p q t j", t=PACK, j=PACK),
+                                        raw[:].rearrange("p j (q t) -> p q t j", t=PACK),
+                                        1.0, 0.0, ALU.mult, ALU.add)
+            else:
+                nc.scalar.copy(tile[:].rearrange("p (t q j) -> p q j t", t=PACK, j=PACK),
+                               raw[:].rearrange("p j (q t) -> p q j t", t=PACK))
+            return tile
+
+        def quantize_weight(raw, name, on_gpsimd=False):
+            return quantize(round_weight(raw, name, on_gpsimd)[:], PASS, name)
+
         def first_stage(name, passes):
-            res = ring.tile([P, S], F32, name=name, tag="res", bufs=RES_BUFS, align_bytes=64)
-            for h in range(2):
-                cols = slice(512 * h, 512 * (h + 1))
-                bank = psum.tile([P, 512], F32, name=name + "_bank", tag="bank")
-                for i, (w, ws, v, vs) in enumerate(passes):
-                    nc.tensor.matmul_mx(out=bank[:], lhsT=w, lhsT_scale=ws, rhs=v[:, cols].bitcast(FP8X4),
-                                        rhs_scale=vs[:, cols], start=(i == 0), stop=(i == len(passes) - 1))
-                nc.scalar.copy(res[:, cols], bank[:])
-            return res
+            result = ring.tile([P, PICKS], F32, name=name, tag="result", bufs=RESULT_BUFS, align_bytes=ALIGN)
+            for col in range(0, PICKS, BANK):
+                cols = slice(col, col + BANK)
+                bank = psum.tile([P, BANK], F32, name=name + "_bank", tag="bank")
+                for i, (weight, weight_scales, words, scales) in enumerate(passes):
+                    nc.tensor.matmul_mx(out=bank[:], lhsT=weight, lhsT_scale=weight_scales,
+                                        rhs=words[:, cols].bitcast(FP8X4), rhs_scale=scales[:, cols],
+                                        start=(i == 0), stop=(i == len(passes) - 1))
+                nc.scalar.copy(result[:, cols], bank[:])
+            return result
 
-        def load_planes(queue, dst, src):
-            for q in range(4):
-                queue.dma_start(dst[32 * q : 32 * q + 4, :].bitcast(I32).rearrange("r (a c) -> r a c", a=2),
-                                src[:, 4 * q : 4 * q + 4, :].bitcast(I32).rearrange("a r c -> r a c"))
+        def fp8_slice(chunk, t):
+            codes, scales = chunk
+            return codes[:, P * t : P * (t + 1)].bitcast(FP8X4), scales[:, P * t : P * (t + 1)]
 
-        warm = keep.tile([P, 1], F32, name="warm")
-        nc.vector.memset(warm[:], 1.0)
-        nc.scalar.activation(warm[:], warm[:], ACT.Sqrt)
-        s2_win = zeroed(T, "s2_win")
-        s1_win = zeroed(T, "s1_win")
-        s3_win = zeroed(T, "s3_win")
-        ws_raw = zeroed(3072, "ws_raw")
-        v_sc1 = zeroed(S, "v_sc1")
-        l_offs2 = load_list(offs2, "l_offs2")
-        wl_raw0 = load_raw(wl[:, 0:512], "wl_raw0")
-        load_scale_rows(nc.sync, s2_win, 0, tab2_scales)
-        w2_win = load_words(tab2_words[0], "w2_win", 0)
-        l_offs = load_list(offs, "l_offs")
-        load_scale_rows(nc.sync, s1_win, 0, tab_scales)
-        wl_raw1 = load_raw(wl[:, 512:1024], "wl_raw1")
-        l_pos2 = load_list(pos2, "l_pos2")
-        l_offs3 = load_list(offs3, "l_offs3")
-        wk_raw = ring.tile([P, 2, 2048], U8, name="wk_raw", tag="y", bufs=2, align_bytes=64)
-        nc.sync.dma_start(wk_raw[:].bitcast(I32), wk_words.rearrange("a p c -> p a c").bitcast(I32))
-        load_planes(nc.sync, ws_raw[:, 0:2048], wk_scales)
-        w1_win0 = load_words(tab_words[0], "w1_win0", 1)
-        wl_bf0 = round_weight(wl_raw0, "wl0", W_ENG[0])
-        wl_q = [quantize(wl_bf0[:], "wl0", 512)]
-        v2_sc = gather_bytes(s2_win, l_offs2, "v2_sc")
-        v2 = gather_words(w2_win, l_offs2, "v2")
-        v_sc0 = gather_bytes(s1_win, l_offs, "v_sc0")
-        shifted(v_sc1, v_sc0, 4)
-        load_planes(nc.sync, ws_raw[:, 2048:3072], wt_scales)
-        w1_win1 = load_words(tab_words[1], "w1_win1", 2)
-        l_pos1 = load_list(pos1, "l_pos1")
-        load_scale_rows(nc.sync, s3_win, 0, tab3_scales)
-        we_raw = [load_raw(we[:, 0:512], "we_raw0")]
-        wl_bf1 = round_weight(wl_raw1, "wl1", W_ENG[1])
-        wl_q.append(quantize(wl_bf1[:], "wl1", 512))
-        wk_dealt = keep.tile([P, 4096], U8, name="wk_dealt", align_bytes=64)
-        deal(wk_dealt[:], wk_raw[:].rearrange("p a c -> p (a c)"), 4)
-        ws_dealt = keep.tile([P, 3072], U8, name="ws_dealt", align_bytes=64)
-        nc.vector.tensor_copy(ws_dealt[:].rearrange("p (b t q) -> p b t q", b=6, t=4),
-                              ws_raw[:].rearrange("p (b q t) -> p b t q", b=6, t=4))
-        w3_win = load_words(tab3_words[0], "w3_win", 0)
-        we_raw.append(load_raw(we[:, 512:1024], "we_raw1"))
-        l_pos3 = load_list(pos3, "l_pos3")
-        wt_raw = ring.tile([P, 2, 1024], U8, name="wt_raw", tag="y", bufs=2, align_bytes=64)
-        nc.sync.dma_start(wt_raw[:].bitcast(I32), wt_words.rearrange("a p c -> p a c").bitcast(I32))
+        def fp4_slice(words, scales, place):
+            return words[:, 2 * P * place : 2 * P * (place + 1)].bitcast(FP4X4), scales[:, P * place : P * (place + 1)]
 
-        def plain_pass(wq, s, v, vs):
-            codes, scales = wq[s // 4]
-            cols = slice(128 * (s % 4), 128 * (s % 4 + 1))
-            return [(codes[:, cols].bitcast(FP8X4), scales[:, cols], v, vs)]
+        tab2_scale_window = zeroed(TABLE, "tab2_scale_window")
+        tab_scale_window = zeroed(TABLE, "tab_scale_window")
+        tab3_scale_window = zeroed(TABLE, "tab3_scale_window")
+        wk_planes = zeroed(2 * wk_scales.shape[2], "wk_planes")
+        wt_planes = zeroed(2 * wt_scales.shape[2], "wt_planes")
+        v_scales1 = zeroed(PICKS, "v_scales1")
 
-        prod = [keep.tile([P, 4, NJ], F32, name="prod0", align_bytes=64)]
-        v1 = []
+        offs2_list = load_list(offs2, "offs2_list")
+        offs_list = load_list(offs, "offs_list")
+        wt_raw = load_fp4(wt_words, "wt_raw")
+        load_plane(tab2_scale_window, tab2_scales)
+        load_planes_stacked(tab_scale_window, tab_scales)
+        offs3_list = load_list(offs3, "offs3_list")
+        load_plane(tab3_scale_window, tab3_scales)
+        wl_raw = [load_weight(wl[:, 0:PASS], "wl_raw0")]
+        load_planes_beside(wt_planes, wt_scales)
+        tab2_window = load_window(tab2_words[0], "tab2_window", 0)
+        wk_raw = load_fp4(wk_words, "wk_raw")
+        load_planes_beside(wk_planes, wk_scales)
+        pos2_list = load_list(pos2, "pos2_list")
+        wl_raw.append(load_weight(wl[:, PASS : 2 * PASS], "wl_raw1"))
+        tab_windows = [load_window(tab_words[0], "tab_window0", 1)]
+
+        wt_dealt = deal(wt_raw[:].rearrange("p a c -> p (a c)"), U16, "wt_dealt")
+        v2_scales = gather_bytes(tab2_scale_window, offs2_list, "v2_scales")
+        v_scales0 = gather_bytes(tab_scale_window, offs_list, "v_scales0")
+        v3_scales = gather_bytes(tab3_scale_window, offs3_list, "v3_scales")
+        wl_q = [quantize_weight(wl_raw[0], "wl0")]
+        wt_scales_dealt = deal(wt_planes[:], U8, "wt_scales_dealt")
+        v2 = gather_words(tab2_window, offs2_list, "v2")
+        nc.sync.dma_start(v_scales1[0 : P - PASS1_ROWS, :].bitcast(I32), v_scales0[PASS1_ROWS:P, :].bitcast(I32))
+
+        tab_windows.append(load_window(tab_words[1], "tab_window1", 2))
+        pos1_list = load_list(pos1, "pos1_list")
+        we_raw = [load_weight(we[:, 0:PASS], "we_raw0")]
+        tab3_window = load_window(tab3_words[0], "tab3_window", 0)
+        wk_dealt = deal(wk_raw[:].rearrange("p a c -> p (a c)"), U16, "wk_dealt")
+        wk_scales_dealt = deal(wk_planes[:], U8, "wk_scales_dealt")
+        wl_q.append(quantize_weight(wl_raw[1], "wl1"))
+        we_raw.append(load_weight(we[:, PASS : 2 * PASS], "we_raw1"))
+        pos3_list = load_list(pos3, "pos3_list")
+
+        product = [keep.tile([P, PACK, JOINED], F32, name="product0", align_bytes=ALIGN)]
+
         def pick_b(s):
-            res = first_stage("b%d" % s, plain_pass(wl_q, s, v2, v2_sc))
-            nc.vector.tensor_copy(prod[s // 4][:, s % 4, :], res[:].indirect(l_pos2[:]))
+            result = first_stage("b%d" % s, [fp8_slice(wl_q[s // PACK], s % PACK) + (v2, v2_scales)])
+            nc.vector.tensor_copy(product[s // PACK][:, s % PACK, :], result[:].indirect(pos2_list[:]))
 
-        for s in range(4):
+        for s in range(PACK):
             pick_b(s)
-        v1.append(gather_words(w1_win0, l_offs, "v1_0"))
-        v1.append(gather_words(w1_win1, l_offs, "v1_1"))
-        prod.append(placed.tile([P, 4, NJ], F32, name="prod1", align_bytes=64, offset=28672))
-        for s in range(4, 8):
+        v = [gather_words(window, offs_list, "v%d_words" % g) for g, window in enumerate(tab_windows)]
+        product.append(placed.tile([P, PACK, JOINED], F32, name="product1", align_bytes=ALIGN,
+                                   offset=2 * WINDOW_BYTES - 2 * PICKED_BYTES))
+        for s in range(PACK, SLICES):
             pick_b(s)
-        we_q = [quantize(round_weight(we_raw[0], "we0", W_ENG[2])[:], "we0", 512)]
-        wy_raw = [load_raw(wy[512 * a : 512 * (a + 1), :], "wy_raw%d" % a) for a in range(2)]
+        we_q = [quantize_weight(we_raw[0], "we0", on_gpsimd=True)]
+        wy_raw = [load_weight(wy[PASS * g : PASS * (g + 1), :], "wy_raw%d" % g) for g in range(2)]
 
-        def a_passes(s):
-            out = []
-            for a in range(2):
-                first = 2048 * a + 256 * s
-                plane = ws_dealt[:, 1024 * a : 1024 * (a + 1)]
-                out.append((wk_dealt[:, first : first + 256].bitcast(FP4X4), plane[:, 128 * s : 128 * (s + 1)],
-                            v1[a], (v_sc0, v_sc1)[a]))
-            return out
+        roots = []
+        d = []
 
-        picked = {}
-        d_res = {}
-        wy_q = []
+        def pick_a(s, tile):
+            passes = [fp4_slice(wk_dealt, wk_scales_dealt, SLICES * g + s) + (v[g], (v_scales0, v_scales1)[g])
+                      for g in range(2)]
+            nc.vector.tensor_copy(tile[:], first_stage("a%d" % s, passes)[:].indirect(pos1_list[:]))
+            roots.append(tile)
 
-        def pick_a(s):
-            res = first_stage("a%d" % s, a_passes(s))
-            picked[s] = ring.tile([P, NJ], F32, name="ga%d" % s, tag="ga", bufs=GA_BUFS, align_bytes=64)
-            nc.vector.tensor_copy(picked[s][:], res[:].indirect(l_pos1[:]))
+        def take_root(s):
+            nc.scalar.activation(roots[s][:], roots[s][:], ACT.Abs)
+            nc.scalar.activation(roots[s][:], roots[s][:], ACT.Sqrt, bias=1.0)
 
-        def root(s):
-            nc.scalar.activation(picked[s][:], picked[s][:], ACT.Abs)
-            nc.scalar.activation(picked[s][:], picked[s][:], ACT.Sqrt, bias=1.0)
+        def multiply(s):
+            picked_b = product[s // PACK][:, s % PACK, :]
+            nc.gpsimd.tensor_tensor(picked_b, picked_b, roots[s][:], ALU.mult)
 
-        def mult(s):
-            dst = prod[s // 4][:, s % 4, :]
-            eng = nc.vector if MULT_ENG == "v" else nc.gpsimd
-            eng.tensor_tensor(dst, dst, picked[s][:], ALU.mult)
+        def pick_d(tile, s, first, width):
+            entries = pos3_list[:, first // 16 : (first + width) // 16]
+            nc.vector.tensor_copy(tile[:, s % PACK, :], d[s][:].indirect(entries))
 
-        def make_d(s):
-            d_res[s] = first_stage("d%d" % s, plain_pass(we_q, s, v3, v3_sc))
+        def subtract(tile, picked_d, g, first, width):
+            nc.vector.tensor_tensor(
+                tile[:].rearrange("p (c i) t -> p c t i", i=2),
+                product[g][:, :, first : first + width].rearrange("p t (c i) -> p c t i", i=2),
+                picked_d[:].rearrange("p t (c i) -> p c t i", i=2), ALU.subtract)
 
-        def make_wy(a):
-            wy_q.append(quantize(round_weight(wy_raw[a], "wy%d" % a, W_ENG[4 + a])[:], "wy%d" % a, 512))
+        pick_a(0, keep.tile([P, JOINED], F32, name="root0", align_bytes=ALIGN))
+        v3 = gather_words(tab3_window, offs3_list, "v3")
+        for s in range(1, SLICES):
+            pick_a(s, placed.tile([P, JOINED], F32, name="root%d" % s, align_bytes=ALIGN, offset=PICKED_BYTES * s))
+            if s + 1 == PACK:
+                take_root(0)
+                multiply(0)
+        we_q.append(quantize_weight(we_raw[1], "we1"))
+        wy_q = [quantize_weight(wy_raw[0], "wy0", on_gpsimd=True)]
 
-        gd_tiles = {}
-
-        def pick_d(s, first, w):
-            key = (s // 4, first)
-            if key not in gd_tiles:
-                gd_tiles[key] = ring.tile([P, 4, w], F32, name="gd%d_%d" % key, tag="gd0" if w == 512 else "gdp",
-                                          bufs=1 if w == 512 else 1, align_bytes=64)
-            nc.vector.tensor_copy(gd_tiles[key][:, s % 4, :],
-                                  d_res[s][:].indirect(l_pos3[:, first // 16 : (first + w) // 16]))
-
-        def join(g, first, w):
-            gd = gd_tiles[(g, first)]
-            zbf = ring.tile([P, w, 4], BF16, name="zbf%d_%d" % (g, first), tag="wbf", bufs=2, align_bytes=64)
-            if SUB_ENG == "v":
-                nc.vector.tensor_tensor(
-                    zbf[:].rearrange("p (c i) t -> p c t i", i=2),
-                    prod[g][:, :, first : first + w].rearrange("p t (c i) -> p c t i", i=2),
-                    gd[:].rearrange("p t (c i) -> p c t i", i=2), ALU.subtract)
-            else:
-                nc.gpsimd.tensor_tensor(gd[:], prod[g][:, :, first : first + w], gd[:], ALU.subtract)
-                nc.scalar.copy(zbf[:].rearrange("p (c i) t -> p c t i", i=4),
-                               gd[:].rearrange("p t (c i) -> p c t i", i=4))
-            return zbf
-
-        def quantize_z(zbf, g, first, w):
-            return quantize(zbf[:].rearrange("p j t -> p (j t)"), "z%d_%d" % (g, first), w)
-
-        wt_dealt = keep.tile([P, 2048], U8, name="wt_dealt", align_bytes=64)
-        y_codes = keep.tile([P, NJ], U32, name="y_codes", align_bytes=64)
-        y_scales = keep.tile([P, NJ], U8, name="y_scales", align_bytes=64)
-        y_rows = out_0.rearrange("(p t) j -> p t j", t=4)
-        words_out = out_1[0].rearrange("p j t -> p (j t)").bitcast(I32)
-
-        banks = {}
-
-        def second_passes(part, w, g, codes, scales, col):
-            per_bank = 512 // w
-            for t0 in range(0, 4, per_bank):
-                if g == 0:
-                    banks[(part, t0)] = (psum.tile([P, 512], F32, name="bent", tag="bank"),
-                                         psum.tile([P, 512], F32, name="lin", tag="bank"))
-                bent = banks[(part, t0)][0]
-                for t in range(t0, t0 + per_bank):
-                    for c0 in range(0, w, 128):
-                        o = (t - t0) * w + c0
-                        byte = 1024 * g + 256 * t
-                        nc.tensor.matmul_mx(
-                            out=bent[:, o : o + 128], lhsT=wt_dealt[:, byte : byte + 256].bitcast(FP4X4),
-                            lhsT_scale=ws_dealt[:, 2048 + 512 * g + 128 * t : 2048 + 512 * g + 128 * (t + 1)],
-                            rhs=codes[:, col + c0 : col + c0 + 128].bitcast(FP8X4),
-                            rhs_scale=scales[:, col + c0 : col + c0 + 128],
-                            start=(g == 0 and o == 0), stop=(g == 1 and o == 384))
-            for t0 in range(0, 4, per_bank):
-                lin = banks[(part, t0)][1]
-                for t in range(t0, t0 + per_bank):
-                    o = (t - t0) * w
-                    nc.tensor.matmul_mx(
-                        out=lin[:, o : o + w], lhsT=wy_q[g][0][:, 128 * t : 128 * (t + 1)].bitcast(FP8X4),
-                        lhsT_scale=wy_q[g][1][:, 128 * t : 128 * (t + 1)],
-                        rhs=codes[:, col : col + w].bitcast(FP8X4), rhs_scale=scales[:, col : col + w],
-                        start=(g == 0 and o == 0), stop=(g == 1 and o + w == 512))
-
-        def second_stage(part, first, w, last):
-            y = ring.tile([P, 4, w], F32, name="y%d" % part, tag="y", bufs=2, align_bytes=64)
-            per_bank = 512 // w
-            flat = y[:].rearrange("p t j -> p (t j)")
-            for t0 in range(0, 4, per_bank):
-                bent, lin = banks[(part, t0)]
-                cols = slice(t0 * w, t0 * w + 512)
-                nc.scalar.activation(flat[:, cols], bent[:], ACT.Tanh)
-                nc.vector.tensor_tensor(flat[:, cols], lin[:], flat[:, cols], ALU.add)
-            nc.sync.dma_start(y_rows[:, :, first : first + w], y[:])
-            ybf = ring.tile([P, w, 4], BF16, name="ybf%d" % part, tag="ybf", bufs=2, align_bytes=64)
-            dst = ybf[:].rearrange("p (c i) t -> p c t i", i=4)
-            src = y[:].rearrange("p t (c i) -> p c t i", i=4)
-            if last:
-                nc.vector.tensor_copy(dst, src)
-            else:
-                nc.scalar.copy(dst, src)
-            nc.vector.quantize_mx(out=y_codes[:, first : first + w].bitcast(FP8X4),
-                                  scales=y_scales[:, first : first + w],
-                                  in_=ybf[:].rearrange("p j t -> p (j t)"))
-            nc.sync.dma_start(words_out[:, first : first + w], y_codes[:, first : first + w].bitcast(I32))
-
-
-        pick_a(0)
-        pick_a(1)
-        v3_sc = gather_bytes(s3_win, l_offs3, "v3_sc")
-        pick_a(2)
-        pick_a(3)
-        root(0)
-        v3 = gather_words(w3_win, l_offs3, "v3")
-        pick_a(4)
-        root(1)
-        mult(0)
-        pick_a(5)
-        root(2)
-        mult(1)
-        we_q.append(quantize(round_weight(we_raw[1], "we1", W_ENG[3])[:], "we1", 512))
-        root(3)
-        mult(2)
-        make_d(0)
-        pick_d(0, 0, 512)
-        make_d(1)
-        pick_d(1, 0, 512)
-        mult(3)
-        pick_a(6)
-        root(4)
-        make_d(2)
-        pick_d(2, 0, 512)
-        make_d(3)
-        pick_d(3, 0, 512)
-        deal(wt_dealt[:], wt_raw[:].rearrange("p a c -> p (a c)"), 2)
-        pick_a(7)
-        root(5)
-        z0 = quantize_z(join(0, 0, 512), 0, 0, 512)
-        mult(4)
-        make_wy(0)
-        make_d(4)
-        root(6)
-        mult(5)
-        make_d(5)
-        root(7)
-        mult(6)
-        make_d(6)
-        mult(7)
-        make_d(7)
-        make_wy(1)
+        picked_d0 = keep.tile([P, PACK, JOINED], F32, name="picked_d0", align_bytes=ALIGN)
+        for s in range(SLICES):
+            if s + 1 < SLICES:
+                take_root(s + 1)
+            d.append(first_stage("d%d" % s, [fp8_slice(we_q[s // PACK], s % PACK) + (v3, v3_scales)]))
+            if s < PACK:
+                pick_d(picked_d0, s, 0, JOINED)
+            if s + 1 < SLICES:
+                multiply(s + 1)
+        z0_rounded = ring.tile([P, JOINED, PACK], BF16, name="z0_rounded", tag="rounded", align_bytes=ALIGN)
+        subtract(z0_rounded, picked_d0, 0, 0, JOINED)
+        z0 = quantize(z0_rounded[:].rearrange("p j t -> p (j t)"), JOINED, "z0")
+        wy1_rounded = round_weight(wy_raw[1], "wy1", False)
+        wy_q.append(quantize(wy1_rounded[:], PASS, "wy1"))
 
         starts = [sum(PARTS[:i]) for i in range(len(PARTS))]
-        for part, w in enumerate(PARTS):
-            second_passes(part, w, 0, z0[0], z0[1], starts[part])
-        for s in range(4, 8):
-            pick_d(s, 0, PARTS[0])
-        for part, w in enumerate(PARTS):
-            more = part + 1 < len(PARTS)
-            zbf = join(1, starts[part], w)
-            if more:
-                pick_d(4, starts[part + 1], PARTS[part + 1])
-            z1 = quantize_z(zbf, 1, starts[part], w)
-            second_passes(part, w, 1, z1[0], z1[1], 0)
-            if more:
-                for s in range(5, 8):
-                    pick_d(s, starts[part + 1], PARTS[part + 1])
-            if part >= 1:
-                second_stage(part - 1, starts[part - 1], PARTS[part - 1], False)
-        second_stage(len(PARTS) - 1, starts[-1], PARTS[-1], True)
-        for q in range(4):
-            queue = nc.sync if q % 2 == 0 else nc.scalar
-            queue.dma_start(out_2[0, 4 * q : 4 * q + 4, :].bitcast(I32), y_scales[32 * q : 32 * q + 4, :].bitcast(I32))
+        banks = {}
+
+        def second_stage(part, g, z, col):
+            width = PARTS[part]
+            codes, scales = z
+            per_bank = BANK // width
+            for t0 in range(0, PACK, per_bank):
+                if g == 0:
+                    banks[(part, t0)] = (psum.tile([P, BANK], F32, name="bent", tag="bank"),
+                                         psum.tile([P, BANK], F32, name="linear", tag="bank"))
+                for t in range(t0, t0 + per_bank):
+                    weight, weight_scales = fp4_slice(wt_dealt, wt_scales_dealt, PACK * g + t)
+                    for c in range(0, width, FP4_N):
+                        at = (t - t0) * width + c
+                        cols = slice(col + c, col + c + FP4_N)
+                        nc.tensor.matmul_mx(out=banks[(part, t0)][0][:, at : at + FP4_N],
+                                            lhsT=weight, lhsT_scale=weight_scales,
+                                            rhs=codes[:, cols].bitcast(FP8X4), rhs_scale=scales[:, cols],
+                                            start=(g == 0 and at == 0), stop=(g == 1 and at + FP4_N == BANK))
+            for t0 in range(0, PACK, per_bank):
+                for t in range(t0, t0 + per_bank):
+                    weight, weight_scales = fp8_slice(wy_q[g], t)
+                    at = (t - t0) * width
+                    cols = slice(col, col + width)
+                    nc.tensor.matmul_mx(out=banks[(part, t0)][1][:, at : at + width],
+                                        lhsT=weight, lhsT_scale=weight_scales,
+                                        rhs=codes[:, cols].bitcast(FP8X4), rhs_scale=scales[:, cols],
+                                        start=(g == 0 and at == 0), stop=(g == 1 and at + width == BANK))
+
+        for part in range(len(PARTS)):
+            second_stage(part, 0, z0, starts[part])
+
+        picked_d1 = [ring.tile([P, PACK, width], F32, name="picked_d1_%d" % part, tag="picked_d1", align_bytes=ALIGN)
+                     for part, width in enumerate(PARTS)]
+        for s in range(PACK, SLICES):
+            pick_d(picked_d1[0], s, 0, PARTS[0])
+        for part, width in enumerate(PARTS):
+            later = part + 1 < len(PARTS)
+            z1_rounded = ring.tile([P, width, PACK], BF16, name="z1_rounded%d" % part, tag="z1_rounded",
+                                   bufs=len(PARTS), align_bytes=ALIGN)
+            subtract(z1_rounded, picked_d1[part], 1, starts[part], width)
+            if later:
+                pick_d(picked_d1[part + 1], PACK, starts[part + 1], PARTS[part + 1])
+            z1 = quantize(z1_rounded[:].rearrange("p j t -> p (j t)"), width, "z1_%d" % part)
+            second_stage(part, 1, z1, 0)
+            if later:
+                for s in range(PACK + 1, SLICES):
+                    pick_d(picked_d1[part + 1], s, starts[part + 1], PARTS[part + 1])
+
+        y_codes = keep.tile([P, JOINED], U32, name="y_codes", align_bytes=ALIGN)
+        y_scales = keep.tile([P, JOINED], U8, name="y_scales", align_bytes=ALIGN)
+        y_rows = out_0.rearrange("(p t) j -> p t j", t=PACK)
+        word_rows = out_1[0].rearrange("p j t -> p (j t)").bitcast(I32)
+        for part, width in enumerate(PARTS):
+            cols = slice(starts[part], starts[part] + width)
+            y = ring.tile([P, PACK, width], F32, name="y%d" % part, tag="y", bufs=len(PARTS), align_bytes=ALIGN)
+            y_flat = y[:].rearrange("p t j -> p (t j)")
+            for t0 in range(0, PACK, BANK // width):
+                bent, linear = banks[(part, t0)]
+                piece = y_flat[:, t0 * width : t0 * width + BANK]
+                nc.scalar.activation(piece, bent[:], ACT.Tanh)
+                nc.vector.tensor_tensor(piece, linear[:], piece, ALU.add)
+            nc.sync.dma_start(y_rows[:, :, cols], y[:])
+            y_rounded = ring.tile([P, width, PACK], BF16, name="y_rounded%d" % part, tag="y_rounded",
+                                  bufs=len(PARTS), align_bytes=ALIGN)
+            interleaved = y_rounded[:].rearrange("p (c i) t -> p c t i", i=4)
+            by_rows = y[:].rearrange("p t (c i) -> p c t i", i=4)
+            if part + 1 < len(PARTS):
+                nc.scalar.copy(interleaved, by_rows)
+            else:
+                nc.vector.tensor_copy(interleaved, by_rows)
+            nc.vector.quantize_mx(out=y_codes[:, cols].bitcast(FP8X4), scales=y_scales[:, cols],
+                                  in_=y_rounded[:].rearrange("p j t -> p (j t)"))
+            nc.sync.dma_start(word_rows[:, cols], y_codes[:, cols].bitcast(I32))
+        for r in range(4):
+            queue = nc.sync if r % 2 == 0 else nc.scalar
+            queue.dma_start(out_2[0, r:16:4, :].bitcast(I32), y_scales[r:P:32, :].bitcast(I32))

@@ -140,6 +140,10 @@ def tile_list_peanut_ejector_join_kernel(
         def fp4_slice(words, scales, place):
             return words[:, 2 * P * place : 2 * P * (place + 1)].bitcast(FP4X4), scales[:, P * place : P * (place + 1)]
 
+        warm = keep.tile([P, 1], F32, name="warm")
+        nc.vector.memset(warm[:], 1.0)
+        nc.scalar.activation(warm[:], warm[:], ACT.Sqrt)
+
         tab2_scale_window = zeroed(TABLE, "tab2_scale_window")
         tab_scale_window = zeroed(TABLE, "tab_scale_window")
         tab3_scale_window = zeroed(TABLE, "tab3_scale_window")
@@ -249,6 +253,7 @@ def tile_list_peanut_ejector_join_kernel(
         z0 = quantize(z0_rounded[:].rearrange("p j t -> p (j t)"), JOINED, "z0")
         wy1_rounded = round_weight(wy_raw[1], "wy1", False)
         wy_q.append(quantize(wy1_rounded[:], PASS, "wy1"))
+        nc.scalar.activation(warm[:], wy1_rounded[:, 0:1], ACT.Tanh)
 
         starts = [sum(PARTS[:i]) for i in range(len(PARTS))]
         banks = {}

from contextlib import ExitStack

import concourse.mybir as mybir

F32 = mybir.dt.float32
BF16 = mybir.dt.bfloat16
I32 = mybir.dt.int32
U32 = mybir.dt.uint32
U16 = mybir.dt.uint16
U8 = mybir.dt.uint8
FP8X4 = mybir.dt.float8_e4m3fn_x4
FP4X4 = mybir.dt.float4_e2m1fn_x4
ACT = mybir.ActivationFunctionType
ALU = mybir.AluOpType

FLOPS = 5368709120

P = 128
PACK = 4
PASS = P * PACK
BANK = 512
TABLE = 4096
PICKS = 1024
JOINED = 512
SLICES = 8
FP4_N = 128
PARTS = (256, 128, 128)
PASS1_ROWS = 16

WINDOW_BYTES = TABLE * 4
PICKED_BYTES = JOINED * 4
RESULT_BUFS = 9
RAW_BUFS = 3
ALIGN = 64


def tile_list_peanut_ejector_join_kernel(
    tc, tab_words, tab_scales, tab2_words, tab2_scales, tab3_words, tab3_scales,
    offs, offs2, offs3, pos1, pos2, pos3, wk_words, wk_scales, wl, we, wy, wt_words, wt_scales,
    out_0, out_1, out_2,
):
    nc = tc.nc
    with ExitStack() as ctx:
        keep = ctx.enter_context(tc.tile_pool(name="keep", bufs=1))
        ring = ctx.enter_context(tc.tile_pool(name="ring", bufs=2))
        placed = ctx.enter_context(tc.tile_pool(name="placed", bufs=1))
        psum = ctx.enter_context(tc.psum_pool(name="psum", bufs=8))

        def load_list(src, name):
            tile = keep.tile([P, src.shape[1]], U16, name=name)
            nc.sync.dma_start(tile[:], src)
            return tile

        def zeroed(width, name):
            tile = keep.tile([P, width], U8, name=name, align_bytes=ALIGN)
            nc.vector.memset(tile[:].bitcast(I32), 0)
            return tile

        def load_window(words, name, place):
            tile = placed.tile([P, TABLE], I32, name=name, align_bytes=ALIGN, offset=WINDOW_BYTES * place)
            nc.sync.dma_start(tile[:], words.rearrange("p n t -> p (n t)").bitcast(I32))
            return tile

        def load_weight(rows, name):
            tile = ring.tile([P, PACK, PASS], F32, name=name, tag="raw", bufs=RAW_BUFS, align_bytes=ALIGN)
            nc.sync.dma_start(tile[:], rows.rearrange("(p j) c -> p j c", j=PACK))
            return tile

        def load_fp4(words, name):
            tile = ring.tile([P, 2, words.shape[2]], U8, name=name, tag="y", bufs=len(PARTS), align_bytes=ALIGN)
            nc.sync.dma_start(tile[:].bitcast(I32), words.rearrange("a p c -> p a c").bitcast(I32))
            return tile

        def load_plane(tile, scales):
            for r in range(4):
                nc.sync.dma_start(tile[r:P:32, :].bitcast(I32), scales[0, r:16:4, :].bitcast(I32))

        def load_planes_stacked(tile, scales):
            for r in range(4):
                nc.sync.dma_start(tile[r:P:PASS1_ROWS, :].bitcast(I32),
                                  scales[:, r:16:4, :].bitcast(I32).rearrange("a q c -> q a c"))

        def load_planes_beside(tile, scales):
            for r in range(4):
                nc.sync.dma_start(tile[r:P:32, :].bitcast(I32).rearrange("q (a c) -> q a c", a=2),
                                  scales[:, r:16:4, :].bitcast(I32).rearrange("a q c -> q a c"))

        def gather_words(window, entries, name):
            tile = keep.tile([P, PICKS], U32, name=name, align_bytes=ALIGN)
            nc.vector.tensor_copy(tile[:], window[:].bitcast(U32).indirect(entries[:]))
            return tile

        def gather_bytes(window, entries, name):
            tile = keep.tile([P, PICKS], U8, name=name, align_bytes=ALIGN)
            nc.vector.tensor_copy(tile[:], window[:].indirect(entries[:]))
            return tile

        def deal(src, dtype, name):
            tile = keep.tile([P, src.shape[1]], U8, name=name, align_bytes=ALIGN)
            nc.vector.tensor_copy(tile[:].bitcast(dtype).rearrange("p (g t q) -> p g t q", t=PACK, q=P),
                                  src.bitcast(dtype).rearrange("p (g q t) -> p g t q", t=PACK, q=P))
            return tile

        def quantize(rounded, width, name):
            codes = keep.tile([P, width], U32, name=name + "_codes", align_bytes=ALIGN)
            scales = keep.tile([P, width], U8, name=name + "_scales", align_bytes=ALIGN)
            nc.vector.quantize_mx(out=codes[:].bitcast(FP8X4), scales=scales[:], in_=rounded)
            return codes, scales

        def round_weight(raw, name, on_gpsimd):
            tile = ring.tile([P, PACK * PASS], BF16, name=name, tag="rounded", align_bytes=ALIGN)
            if on_gpsimd:
                nc.gpsimd.tensor_scalar(tile[:].rearrange("p (t q j) -> p q t j", t=PACK, j=PACK),
                                        raw[:].rearrange("p j (q t) -> p q t j", t=PACK),
                                        1.0, 0.0, ALU.mult, ALU.add)
            else:
                nc.scalar.copy(tile[:].rearrange("p (t q j) -> p q j t", t=PACK, j=PACK),
                               raw[:].rearrange("p j (q t) -> p q j t", t=PACK))
            return tile

        def quantize_weight(raw, name, on_gpsimd=False):
            return quantize(round_weight(raw, name, on_gpsimd)[:], PASS, name)

        def first_stage(name, passes):
            result = ring.tile([P, PICKS], F32, name=name, tag="result", bufs=RESULT_BUFS, align_bytes=ALIGN)
            for col in range(0, PICKS, BANK):
                cols = slice(col, col + BANK)
                bank = psum.tile([P, BANK], F32, name=name + "_bank", tag="bank")
                for i, (weight, weight_scales, words, scales) in enumerate(passes):
                    nc.tensor.matmul_mx(out=bank[:], lhsT=weight, lhsT_scale=weight_scales,
                                        rhs=words[:, cols].bitcast(FP8X4), rhs_scale=scales[:, cols],
                                        start=(i == 0), stop=(i == len(passes) - 1))
                nc.scalar.copy(result[:, cols], bank[:])
            return result

        def fp8_slice(chunk, t):
            codes, scales = chunk
            return codes[:, P * t : P * (t + 1)].bitcast(FP8X4), scales[:, P * t : P * (t + 1)]

        def fp4_slice(words, scales, place):
            return words[:, 2 * P * place : 2 * P * (place + 1)].bitcast(FP4X4), scales[:, P * place : P * (place + 1)]

        warm = keep.tile([P, 1], F32, name="warm")
        nc.vector.memset(warm[:], 1.0)
        nc.scalar.activation(warm[:], warm[:], ACT.Sqrt)

        tab2_scale_window = zeroed(TABLE, "tab2_scale_window")
        tab_scale_window = zeroed(TABLE, "tab_scale_window")
        tab3_scale_window = zeroed(TABLE, "tab3_scale_window")
        wk_planes = zeroed(2 * wk_scales.shape[2], "wk_planes")
        wt_planes = zeroed(2 * wt_scales.shape[2], "wt_planes")
        v_scales1 = zeroed(PICKS, "v_scales1")

        offs2_list = load_list(offs2, "offs2_list")
        offs_list = load_list(offs, "offs_list")
        wt_raw = load_fp4(wt_words, "wt_raw")
        load_plane(tab2_scale_window, tab2_scales)
        load_planes_stacked(tab_scale_window, tab_scales)
        offs3_list = load_list(offs3, "offs3_list")
        load_plane(tab3_scale_window, tab3_scales)
        wl_raw = [load_weight(wl[:, 0:PASS], "wl_raw0")]
        load_planes_beside(wt_planes, wt_scales)
        tab2_window = load_window(tab2_words[0], "tab2_window", 0)
        wk_raw = load_fp4(wk_words, "wk_raw")
        load_planes_beside(wk_planes, wk_scales)
        pos2_list = load_list(pos2, "pos2_list")
        wl_raw.append(load_weight(wl[:, PASS : 2 * PASS], "wl_raw1"))
        tab_windows = [load_window(tab_words[0], "tab_window0", 1)]

        wt_dealt = deal(wt_raw[:].rearrange("p a c -> p (a c)"), U16, "wt_dealt")
        v2_scales = gather_bytes(tab2_scale_window, offs2_list, "v2_scales")
        v_scales0 = gather_bytes(tab_scale_window, offs_list, "v_scales0")
        v3_scales = gather_bytes(tab3_scale_window, offs3_list, "v3_scales")
        wl_q = [quantize_weight(wl_raw[0], "wl0")]
        wt_scales_dealt = deal(wt_planes[:], U8, "wt_scales_dealt")
        v2 = gather_words(tab2_window, offs2_list, "v2")
        nc.sync.dma_start(v_scales1[0 : P - PASS1_ROWS, :].bitcast(I32), v_scales0[PASS1_ROWS:P, :].bitcast(I32))

        tab_windows.append(load_window(tab_words[1], "tab_window1", 2))
        pos1_list = load_list(pos1, "pos1_list")
        we_raw = [load_weight(we[:, 0:PASS], "we_raw0")]
        tab3_window = load_window(tab3_words[0], "tab3_window", 0)
        wk_dealt = deal(wk_raw[:].rearrange("p a c -> p (a c)"), U16, "wk_dealt")
        wk_scales_dealt = deal(wk_planes[:], U8, "wk_scales_dealt")
        wl_q.append(quantize_weight(wl_raw[1], "wl1"))
        we_raw.append(load_weight(we[:, PASS : 2 * PASS], "we_raw1"))
        pos3_list = load_list(pos3, "pos3_list")

        product = [keep.tile([P, PACK, JOINED], F32, name="product0", align_bytes=ALIGN)]

        def pick_b(s):
            result = first_stage("b%d" % s, [fp8_slice(wl_q[s // PACK], s % PACK) + (v2, v2_scales)])
            nc.vector.tensor_copy(product[s // PACK][:, s % PACK, :], result[:].indirect(pos2_list[:]))

        for s in range(PACK):
            pick_b(s)
        v = [gather_words(window, offs_list, "v%d_words" % g) for g, window in enumerate(tab_windows)]
        product.append(placed.tile([P, PACK, JOINED], F32, name="product1", align_bytes=ALIGN,
                                   offset=2 * WINDOW_BYTES - 2 * PICKED_BYTES))
        for s in range(PACK, SLICES):
            pick_b(s)
        we_q = [quantize_weight(we_raw[0], "we0", on_gpsimd=True)]
        wy_raw = [load_weight(wy[PASS * g : PASS * (g + 1), :], "wy_raw%d" % g) for g in range(2)]

        roots = []
        d = []

        def pick_a(s, tile):
            passes = [fp4_slice(wk_dealt, wk_scales_dealt, SLICES * g + s) + (v[g], (v_scales0, v_scales1)[g])
                      for g in range(2)]
            nc.vector.tensor_copy(tile[:], first_stage("a%d" % s, passes)[:].indirect(pos1_list[:]))
            roots.append(tile)

        def take_root(s):
            nc.scalar.activation(roots[s][:], roots[s][:], ACT.Abs)
            nc.scalar.activation(roots[s][:], roots[s][:], ACT.Sqrt, bias=1.0)

        def multiply(s):
            picked_b = product[s // PACK][:, s % PACK, :]
            nc.gpsimd.tensor_tensor(picked_b, picked_b, roots[s][:], ALU.mult)

        def pick_d(tile, s, first, width):
            entries = pos3_list[:, first // 16 : (first + width) // 16]
            nc.vector.tensor_copy(tile[:, s % PACK, :], d[s][:].indirect(entries))

        def subtract(tile, picked_d, g, first, width):
            nc.vector.tensor_tensor(
                tile[:].rearrange("p (c i) t -> p c t i", i=2),
                product[g][:, :, first : first + width].rearrange("p t (c i) -> p c t i", i=2),
                picked_d[:].rearrange("p t (c i) -> p c t i", i=2), ALU.subtract)

        pick_a(0, keep.tile([P, JOINED], F32, name="root0", align_bytes=ALIGN))
        v3 = gather_words(tab3_window, offs3_list, "v3")
        for s in range(1, SLICES):
            pick_a(s, placed.tile([P, JOINED], F32, name="root%d" % s, align_bytes=ALIGN, offset=PICKED_BYTES * s))
            if s + 1 == PACK:
                take_root(0)
                multiply(0)
        we_q.append(quantize_weight(we_raw[1], "we1"))
        wy_q = [quantize_weight(wy_raw[0], "wy0", on_gpsimd=True)]

        picked_d0 = keep.tile([P, PACK, JOINED], F32, name="picked_d0", align_bytes=ALIGN)
        for s in range(SLICES):
            if s + 1 < SLICES:
                take_root(s + 1)
            d.append(first_stage("d%d" % s, [fp8_slice(we_q[s // PACK], s % PACK) + (v3, v3_scales)]))
            if s < PACK:
                pick_d(picked_d0, s, 0, JOINED)
            if s + 1 < SLICES:
                multiply(s + 1)
        z0_rounded = ring.tile([P, JOINED, PACK], BF16, name="z0_rounded", tag="rounded", align_bytes=ALIGN)
        subtract(z0_rounded, picked_d0, 0, 0, JOINED)
        z0 = quantize(z0_rounded[:].rearrange("p j t -> p (j t)"), JOINED, "z0")
        wy1_rounded = round_weight(wy_raw[1], "wy1", False)
        wy_q.append(quantize(wy1_rounded[:], PASS, "wy1"))
        nc.scalar.activation(warm[:], wy1_rounded[:, 0:1], ACT.Tanh)

        starts = [sum(PARTS[:i]) for i in range(len(PARTS))]
        banks = {}

        def second_stage(part, g, z, col):
            width = PARTS[part]
            codes, scales = z
            per_bank = BANK // width
            for t0 in range(0, PACK, per_bank):
                if g == 0:
                    banks[(part, t0)] = (psum.tile([P, BANK], F32, name="bent", tag="bank"),
                                         psum.tile([P, BANK], F32, name="linear", tag="bank"))
                for t in range(t0, t0 + per_bank):
                    weight, weight_scales = fp4_slice(wt_dealt, wt_scales_dealt, PACK * g + t)
                    for c in range(0, width, FP4_N):
                        at = (t - t0) * width + c
                        cols = slice(col + c, col + c + FP4_N)
                        nc.tensor.matmul_mx(out=banks[(part, t0)][0][:, at : at + FP4_N],
                                            lhsT=weight, lhsT_scale=weight_scales,
                                            rhs=codes[:, cols].bitcast(FP8X4), rhs_scale=scales[:, cols],
                                            start=(g == 0 and at == 0), stop=(g == 1 and at + FP4_N == BANK))
            for t0 in range(0, PACK, per_bank):
                for t in range(t0, t0 + per_bank):
                    weight, weight_scales = fp8_slice(wy_q[g], t)
                    at = (t - t0) * width
                    cols = slice(col, col + width)
                    nc.tensor.matmul_mx(out=banks[(part, t0)][1][:, at : at + width],
                                        lhsT=weight, lhsT_scale=weight_scales,
                                        rhs=codes[:, cols].bitcast(FP8X4), rhs_scale=scales[:, cols],
                                        start=(g == 0 and at == 0), stop=(g == 1 and at + width == BANK))

        for part in range(len(PARTS)):
            second_stage(part, 0, z0, starts[part])

        picked_d1 = [ring.tile([P, PACK, width], F32, name="picked_d1_%d" % part, tag="picked_d1", align_bytes=ALIGN)
                     for part, width in enumerate(PARTS)]
        for s in range(PACK, SLICES):
            pick_d(picked_d1[0], s, 0, PARTS[0])
        for part, width in enumerate(PARTS):
            later = part + 1 < len(PARTS)
            z1_rounded = ring.tile([P, width, PACK], BF16, name="z1_rounded%d" % part, tag="z1_rounded",
                                   bufs=len(PARTS), align_bytes=ALIGN)
            subtract(z1_rounded, picked_d1[part], 1, starts[part], width)
            if later:
                pick_d(picked_d1[part + 1], PACK, starts[part + 1], PARTS[part + 1])
            z1 = quantize(z1_rounded[:].rearrange("p j t -> p (j t)"), width, "z1_%d" % part)
            second_stage(part, 1, z1, 0)
            if later:
                for s in range(PACK + 1, SLICES):
                    pick_d(picked_d1[part + 1], s, starts[part + 1], PARTS[part + 1])

        y_codes = keep.tile([P, JOINED], U32, name="y_codes", align_bytes=ALIGN)
        y_scales = keep.tile([P, JOINED], U8, name="y_scales", align_bytes=ALIGN)
        y_rows = out_0.rearrange("(p t) j -> p t j", t=PACK)
        word_rows = out_1[0].rearrange("p j t -> p (j t)").bitcast(I32)
        for part, width in enumerate(PARTS):
            cols = slice(starts[part], starts[part] + width)
            y = ring.tile([P, PACK, width], F32, name="y%d" % part, tag="y", bufs=len(PARTS), align_bytes=ALIGN)
            y_flat = y[:].rearrange("p t j -> p (t j)")
            for t0 in range(0, PACK, BANK // width):
                bent, linear = banks[(part, t0)]
                piece = y_flat[:, t0 * width : t0 * width + BANK]
                nc.scalar.activation(piece, bent[:], ACT.Tanh)
                nc.vector.tensor_tensor(piece, linear[:], piece, ALU.add)
            nc.sync.dma_start(y_rows[:, :, cols], y[:])
            y_rounded = ring.tile([P, width, PACK], BF16, name="y_rounded%d" % part, tag="y_rounded",
                                  bufs=len(PARTS), align_bytes=ALIGN)
            interleaved = y_rounded[:].rearrange("p (c i) t -> p c t i", i=4)
            by_rows = y[:].rearrange("p t (c i) -> p c t i", i=4)
            if part + 1 < len(PARTS):
                nc.scalar.copy(interleaved, by_rows)
            else:
                nc.vector.tensor_copy(interleaved, by_rows)
            nc.vector.quantize_mx(out=y_codes[:, cols].bitcast(FP8X4), scales=y_scales[:, cols],
                                  in_=y_rounded[:].rearrange("p j t -> p (j t)"))
            nc.sync.dma_start(word_rows[:, cols], y_codes[:, cols].bitcast(I32))
        for r in range(4):
            queue = nc.sync if r % 2 == 0 else nc.scalar
            queue.dma_start(out_2[0, r:16:4, :].bitcast(I32), y_scales[r:P:32, :].bitcast(I32))
